import numpy as np, ml_dtypes
CORES = [3,7,11,15,131,135,139,143]
N = 8
import mx_ref
BF = ml_dtypes.bfloat16
def gcols(t, e):
    v = np.concatenate([t.reshape(8, 16, -1, 4), np.zeros((8, 16, 1, 4), BF)], axis=2)
    return np.ascontiguousarray(np.stack([v[g][:, e[g]] for g in range(8)])).reshape(128, -1)
def tile(rs):
    return np.stack(rs, axis=2).reshape(128, -1).astype(BF)
def pick(q, e):
    c = np.concatenate([q[0].reshape(128, -1, 4), np.zeros((128, 1, 4), np.uint8)], axis=1); s = np.concatenate([q[1], np.ones((16, 1), np.uint8)], axis=1)
    return (np.ascontiguousarray(c[:, e].reshape(128, -1)), np.ascontiguousarray(s[:, e]))
def join(*qs):
    return (np.concatenate([q[0] for q in qs], axis=1), np.concatenate([q[1] for q in qs], axis=1))
def put(q, e, v):
    c, s = q[0].reshape(128, -1, 4).copy(), q[1].copy(); c[:, e] = v[0].reshape(128, -1, 4); s[:, e] = v[1]
    return (c.reshape(128, -1), s)
def pk(c, s):
    return (np.ascontiguousarray(c), mx_ref.live(s))
def emit(q):
    return q[0], q[1]
def packed(v, rng):
    q = [mx_ref.quantize(np.ascontiguousarray(v[r])) for r in range(N)]
    return np.stack([a for a, b in q]), np.stack([mx_ref.plane(b, rng) for a, b in q])
def values_of_codes():
    e, c = np.zeros((128, 128, 4), np.float32), np.zeros((128, 2, 4), np.uint8)
    e[np.arange(128), np.arange(128), 0] = 1
    c[:127, :, 0] = np.arange(256).reshape(2, 128).T[:127]
    return mx_ref.matmul(mx_ref.quantize(e.reshape(128, 512).astype(BF)), (c.reshape(128, 8), np.full((16, 2), 127, np.uint8))).T.reshape(-1).astype(np.float64)
CODE_VALUE, SCALE_VALUE = values_of_codes(), 2.0 ** (np.arange(256) - 127.0)
def decode(q):
    return (CODE_VALUE[q[0]].reshape(16, 8, -1, 4) * SCALE_VALUE[q[1]][:, None, :, None] + 0.0).reshape(128, -1).astype(np.float32)
def f(rng, *shape):
    return mx_ref.flush((rng.standard_normal(shape, dtype=np.float32) * np.exp2(rng.integers(-2, 3, shape[:-1] + (1,)))).astype(BF))
def wide(rng, *shape, cols=0):
    v = rng.standard_normal(shape, dtype=np.float32) * np.exp2(rng.integers(-12, 13, shape)).astype(np.float32)
    if cols: v *= np.repeat(np.exp2(rng.integers(-cols, cols + 1, shape[:-2] + (1, shape[-1] // 4))) * (rng.random(shape[:-2] + (1, shape[-1] // 4)) > 0.0625), 4, axis=-1).astype(np.float32)
    return mx_ref.flush(v.astype(BF))
C, M, R = 128, 48, 3
HALF = np.arange(C) // 2
def order(p):
    return np.argsort(-(p + np.float32(0.0)), axis=1, kind="stable")
def gput(t, e, h):
    a, b = t.reshape(8, 16, -1, 4).copy(), h.reshape(8, 16, -1, 4)
    for g in range(8): a[g][:, e[g]] = b[g]
    return a.reshape(128, -1)
def trials(q, t, o):
    s = []
    for g in range(0, 8, 2):
        e = np.concatenate([np.where(np.arange(8)[:, None] == k, o, o[:, HALF]) for k in (g, g + 1)], axis=1)
        p = mx_ref.matmul(q, mx_ref.quantize(gcols(t, e)))
        s += [p[16 * g, :C], p[16 * g + 16, C:]]
    return np.stack(s)
def big(v):
    v = v.astype(np.float32)
    v[np.abs(v) < np.float32(2.0 ** -16)] = 0
    return v.astype(BF)
def numbers_of(rng):
    return {"x": big(f(rng, N, 128, 4 * C)), "u": np.array(f(rng, N, 128, 512)), "v": np.array(f(rng, N, 128, 512))}
def layers(rng):
    return big(f(rng, N, 128, 2048)).reshape(N, 8, 16, 4, 8, 16, 4)
def weights(rng, w):
    c, p = packed(np.ascontiguousarray(w).reshape(N, 128, 2048), rng)
    return {"wc": c, "ws": p}
def signs(rng):
    return np.stack([rng.permutation(8) % 2 * 2.0 - 1.0 for r in range(N)])
def setup_inputs(rng):
    return {**numbers_of(rng), **weights(rng, layers(rng))}
def setup_inputs_ties(rng):
    d = numbers_of(rng)
    e = rng.permutation(N)
    x = d["x"].reshape(N, 8, 16, C, 4)
    u = d["u"].reshape(N, 8, 16, 128, 4)
    u[:, :, 8:, ::16] = 0
    for r in range(N):
        k = np.zeros(C, int) if r == e[0] else rng.permutation(C) % 3
        a = x[r][:, :8, :3].copy()
        a[:, :, 2] = 0
        x[r][:, :8] = a[:, :, k]
        for g in rng.permutation(8)[:4]: u[r, g, :, 16 * g] = 0
    x[e[1]] = 0
    w = layers(rng)
    w[:, :, :, :, :, :8] = 0
    return {"x": x.reshape(N, 128, 4 * C), "u": u.reshape(N, 128, 512), "v": d["v"], **weights(rng, w)}
def setup_inputs_near(rng):
    d = numbers_of(rng)
    x = d["x"].astype(np.float32).reshape(N, 8, 16, C, 4)
    u = d["u"].reshape(N, 128, 128, 4)
    u[:, :, ::16] = 0
    o, c, j = rng.permutation(N) % 4, signs(rng), np.arange(C)
    upper = j // (C // 2)
    own = np.arange(128)[:, None, None] // 16 == np.arange(8)[:, None]
    for r in range(N):
        if o[r] == 3:
            k = rng.choice([-1.0, 1.0], (128, 8, 4)) * rng.integers(8, 16, (128, 8, 4)) * 0.125
            u[r, :, ::16] = (k * np.where(own, 2.0 ** -18, 1.0)).astype(np.float32).astype(BF)
            continue
        a = rng.integers(0, C, (8, 1))
        s = (j + a) % (C // 2) if o[r] == 2 else (j + a) % C // 2
        size = 2.0 ** -4 if o[r] == 2 else 1.0
        z = ((s[:, :, None] >> np.arange(8)) & 1) * np.exp2(np.arange(8) - 23.0) * size
        x[r] = 0
        if o[r] == 2:
            x[r, :, 0, :, 0] = np.where(c[r][:, None] > 0, (8 + upper) * 2.0 ** -30, 9 * upper * 2.0 ** -33)
            x[r, :, 1, :, 0] = np.where(c[r][:, None] > 0, 0.0, 10 * (1 - upper) * 2.0 ** -33)
        else:
            x[r, :, 0, :, 0] = c[r][:, None]
            for i in rng.permutation(8)[:4]: x[r, i, 0, rng.integers(C), 0] *= np.float32(2.0 ** 30)
        x[r, :, 8] = z[:, :, :4]
        x[r, :, 9] = z[:, :, 4:]
        x[r, :, 10:] = rng.integers(4, 8, (8, 6, C, 4)) * 2.0 ** -20 * size
        k = 1.0 if o[r] == 0 else 2.0 ** -30
        for h in range(0, 128, 16):
            u[r, h, h, 0] = k
            u[r, h + 8:h + 10, h] = k
            if o[r] == 2 and c[r, h // 16] < 0:
                u[r, h, h, 0] = 9 * 2.0 ** -33
                u[r, h + 1, h, 0] = 2.0 ** -30
    w = layers(rng)
    w[:, :, :10] = 0
    w[:, :, :, :, :, :10] = 0
    return {"x": x.reshape(N, 128, 4 * C).astype(BF), "u": u.reshape(N, 128, 512), "v": d["v"], **weights(rng, w)}
def setup_inputs_huge(rng):
    d = numbers_of(rng)
    c = np.stack([rng.permutation(C) % 2 * 2.0 - 1.0 for r in range(N)])
    c[rng.permutation(N) < N // 2] = -1
    x = (0.6 + 0.2 * rng.random((N, 128, C, 4))) * np.where(c < 0, -2.0 ** 30, 2.0 ** 28)[:, None, :, None]
    u = d["u"].reshape(N, 128, 128, 4)
    s = signs(rng)
    a = 2.0 ** 30 * (1 - 0.25 * rng.random((N, 128, 8, 4))) * s[:, None, :, None]
    for r in range(N):
        if (c[r] < 0).all():
            x[r, :, rng.integers(C)] = -2.0 ** 30
            a[r, :, rng.choice(np.flatnonzero(s[r] > 0))] = 2.0 ** 30
    u[:, :, ::16] = a.astype(np.float32).astype(BF)
    w = np.zeros((N, 128, 4, 128, 4), np.float32)
    i = np.arange(128)
    for b in range(4): w[:, i, b, i, b] = 16
    return {"x": x.astype(np.float32).reshape(N, 128, 4 * C).astype(BF), "u": u.reshape(N, 128, 512), "v": d["v"], **weights(rng, w.astype(BF))}
def setup_inputs_twice(rng):
    d = numbers_of(rng)
    e = 2 + np.arange(32).reshape(8, 4) // 2
    n = (N, 16, 8, C, 4)
    x = rng.choice([-1.0, 1.0], n) * (9 + 2 * rng.integers(0, 4, n)) * 0.125 * np.exp2(0.0 - e)[:, None]
    x[:, :, 0] = 0
    x[:, :, 0, :, 0] = 1.96875 * rng.choice([-1.0, 1.0], (N, 16, C))
    x *= np.exp2(rng.integers(1, 5, (N, 16, 1, C, 1)))
    u = d["u"].reshape(N, 16, 8, 128, 4)
    k = rng.choice([-1.0, 1.0], (N, 16, 8, 8, 4)) * rng.integers(8, 16, (N, 16, 8, 8, 4)) * 0.125 * np.exp2(e - 17.0)[:, None]
    k[:, :, 0] = 0
    u[:, :, :, ::16] = k.astype(np.float32).astype(BF)
    return {"x": x.astype(np.float32).reshape(N, 128, 4 * C).astype(BF), "u": u.reshape(N, 128, 512), "v": d["v"], **weights(rng, layers(rng))}
def setup_inputs_spread(rng):
    d = setup_inputs(rng)
    d["x"] = big(wide(rng, N, 128, 4 * C, cols=6))
    return d
def check_inputs(d):
    b = []
    for k in ("x", "u", "v"):
        a = np.abs(d[k].astype(np.float32))
        if not (np.isfinite(a).all() and ((a == 0) | (a >= 2.0 ** -30) & (a <= 2.0 ** 30)).all()): b.append("a value of " + k)
    none, least, most = [emit(mx_ref.quantize(np.full((128, 16), k, np.float32).astype(BF)))[1][0, 0] for k in (0.0, 2.0 ** -30, 2.0 ** 30)]
    for r in range(N):
        if ((d["wc"][r] == 0x7F) | (d["wc"][r] == 0xFF)).any(): b.append("wc: a code that is no number")
        s = mx_ref.live(d["ws"][r])
        if ((s != none) & ((s < least) | (s > most))).any(): b.append("ws: a scale out of range")
    return b
def reference(x, u, v, wc, ws):
    qu = [mx_ref.quantize(u[r]) for r in range(N)]
    lay = [pk(wc[r], ws[r]) for r in range(N)]
    now = [x[r] for r in range(N)]
    o = [order(mx_ref.matmul(qu[r], mx_ref.quantize(x[r]))[::16]) for r in range(N)]
    for t in range(R):
        sent = []
        for r in range(N):
            now[r] = decode(mx_ref.quantize(now[r])).astype(BF)
            score = np.zeros((8, C), np.float32)
            np.put_along_axis(score, o[r], trials(qu[r], now[r], o[r]), axis=1)
            o[r] = order(score)
            sent.append(mx_ref.quantize(gcols(now[r], o[r][:, :M])))
        for r in range(N):
            q = sent[(r - 1 - t) % N]
            c = decode(q)
            h = tile([np.maximum(mx_ref.matmul(pick(lay[r], np.arange(128 * b, 128 * b + 128)), q), np.float32(0.0)) * np.float32(0.03125) + c[:, b::4] for b in range(4)])
            now[r] = gput(now[r], o[r][:, C - M:], h)
    y, ol = np.zeros((N, 128, C), np.float32), np.zeros((N, 8, C), np.float32)
    oc, osc = np.zeros((N, 128, 4 * C), np.uint8), np.zeros((N, 16, C), np.uint8)
    for r in range(N):
        q = mx_ref.quantize(now[r])
        y[r] = mx_ref.matmul(mx_ref.quantize(v[r]), q)
        ol[r] = o[r]
        oc[r], osc[r] = emit(q)
    return {"y": y, "ol": ol, "oc": oc, "osc": osc}

from concourse.bass import DstId, RemoteDMATransfer
from concourse.mybir import dt, AluOpType, ActivationFunctionType

C, M, ROUNDS = 128, 48, 3
KEEP = C - M
NA = 32
KA = 4
NV = 7
CUT = 256
BIG = 1.0e25
F32, BF, I32, U16, Q4, U8 = "float32", "bfloat16", "int32", "uint16", "float8_e4m3fn_x4", "uint8"

SCRATCH = {}
for _n, _w, _d in [
    ("xs", 512, BF), ("us", 512, BF), ("vs", 512, BF),
    ("wq", 512, Q4), ("wp", 512, U8), ("uq", 128, Q4), ("up", 128, U8), ("ubq", 128, Q4), ("ubp", 128, U8),
    ("vq", 128, Q4), ("vp", 128, U8), ("xq", 128, Q4), ("xp", 128, U8),
    ("et", 520, BF), ("eq", 512, Q4), ("ep", 512, U8), ("gt", 512, BF), ("gq", 128, Q4), ("gp", 128, U8),
    ("u0", 512, BF), ("ust", 512, BF), ("st", 512, BF), ("fin", 512, BF),
    ("sq", 128, Q4), ("sp", 192, U8), ("hq", 128, Q4), ("hp", 128, U8), ("fq", 128, Q4), ("fp", 128, U8),
    ("lq0", 176, Q4), ("lp0", 320, U8), ("lq1", 176, Q4), ("lp1", 320, U8), ("lq2", 176, Q4), ("lp2", 320, U8),
    ("ya", 1024, BF), ("yb", 1536, BF), ("yc", 1536, BF), ("yq", 1024, Q4), ("yp", 1024, U8),
    ("ps", 1024, F32), ("sc", 128, F32), ("xm", 128, F32), ("own", 128, F32),
    ("bt", 1024, BF), ("bq", 256, Q4), ("bp", 256, U8), ("junk", 896, BF), ("off", 8, F32),
    ("dsc", 128, F32), ("sel", 128, F32), ("rs", 8, F32), ("rr", 8, F32),
    ("m1", 8, F32), ("m2", 8, F32), ("m3", 8, F32), ("m4", 8, F32),
    ("lr", 8, U16), ("la", 8, U16), ("l32", 32, U16), ("lf", 32, U16), ("lu", 8, U16), ("lsc", 12, U16), ("lya", 64, U16),
    ("va", 128, F32), ("vb", 128, F32), ("wb", 128, F32), ("s4", 128, F32), ("ob", 128, F32),
    ("rl", 192, F32), ("ysb", 128, F32),
    ("ip", 1, I32), ("ci", 8, I32), ("cf", 8, F32), ("cd", 16, F32), ("i16", 12, F32),
    ("jm", 128, BF), ("kk", 128, BF), ("kc", 128, F32), ("dd", 128, BF), ("i4", 128, F32), ("j4", 128, BF),
    ("mp", 128, F32), ("ko", 128, F32), ("k16", 128, F32), ("k4a", 128, F32), ("k4", 128, F32),
    ("i4t", 128, F32), ("ic", 128, F32), ("t1", 64, F32), ("t2", 64, F32), ("t3", 64, F32), ("t4", 64, F32), ("t5", 64, F32),
]:
    SCRATCH[_n] = ("sbuf", [128, _w], _d)
SCRATCH["dup"] = ("sbuf", [128, 96, 4], BF)
for _b in range(8):
    SCRATCH["p%d" % _b] = ("psum", [128, 512], F32)

SEMAPHORES = ["cv", "ca", "ct", "cg", "dx", "du", "dv", "dwq", "dwp", "dpad", "dout", "sent", "arr0", "arr1", "arr2"]

A_ = AluOpType
AF = ActivationFunctionType


def rank_program(g, core, T, topo):
    rank = T.rank_of(core)
    if rank is None:
        return
    n = len(T.cores)
    Q = {"v": g.vector, "a": g.scalar, "t": g.tensor, "g": g, "s": g.sync}
    own_sem = {"v": "cv", "a": "ca", "t": "ct", "g": "cg"}
    count = {}
    known = {q: {} for q in Q}
    writer, readers = {}, {}

    def need(q, tok):
        sem, val, snap = tok[0], tok[1], tok[2]
        if known[q].get(sem, 0) >= val:
            return
        Q[q].wait_ge(T.sem[sem], val)
        known[q][sem] = val
        for s, x in snap.items():
            if known[q].get(s, 0) < x:
                known[q][s] = x

    def op(q, fn, R=(), W=(), X=(), dma=None, ext=(), remote=None):
        deps = []
        for k in R:
            if k in writer:
                deps.append(writer[k])
        for k in W:
            deps += readers.get(k, []) + ([writer[k]] if k in writer else [])
        for k in X:
            if k in writer and writer[k][3] != q:
                deps.append(writer[k])
        for sem, val in ext:
            deps.append((sem, val, {}, None))
        deps.sort(key=lambda d: -d[1])
        for tok in deps:
            need(q, tok)
        ins = fn()
        if remote is not None:
            sem, step, who = remote[0], remote[1], None
        elif dma is not None:
            sem, step, who = dma, 16, None
            ins.then_inc(T.sem[sem], step)
        else:
            sem, step, who = own_sem[q], 1, q
            ins.then_inc(T.sem[sem], step)
        count[sem] = count.get(sem, 0) + step
        tok = (sem, count[sem], dict(known[q]), who)
        for k in R:
            readers.setdefault(k, []).append(tok)
        for k in list(W) + list(X):
            writer[k] = tok
            readers[k] = []

    V, S = g.vector, g.scalar
    P = [T["p%d" % b] for b in range(8)]

    def ts(out, in0, s1, o0, s2=None, o1=None, R=(), W=(), X=()):
        if o1 is None:
            op("v", lambda: V.tensor_scalar(out, in0, s1, None, o0), R, W, X)
        else:
            op("v", lambda: V.tensor_scalar(out, in0, s1, s2, o0, o1), R, W, X)

    def tt(out, a, b, o, R=(), W=(), X=()):
        op("v", lambda: V.tensor_tensor(out, a, b, o), R, W, X)

    def scan(out, d0, d1, o0, o1, R=(), W=(), X=()):
        op("v", lambda: V.tensor_tensor_scan(out, d0, d1, 0.0, o0, o1), R, W, X)

    def cp(q, out, in_, R=(), W=(), X=()):
        if q == "v":
            op("v", lambda: V.tensor_copy(out, in_), R, W, X)
        elif q == "a":
            op("a", lambda: S.activation(out, in_, AF.Copy), R, W, X)
        else:
            w = 1
            for d in list(out.shape)[1:]:
                w *= int(d)
            op("g", lambda: g.affine_select(out, in_, [[0, w]], A_.is_ge, 0.0, 0, 0), R, W, X)

    def lin(out, in_, scale, bias, R, W):
        op("a", lambda: S.activation(out, in_, AF.Identity, bias=bias, scale=scale), R, W)

    def quant(cq, cs, in_, R=(), W=()):
        op("v", lambda: V.quantize_mx(cq, cs, in_), R, W)

    def mm(b, w, lq, lp, rq, rp, R, start=True, stop=True, ext=()):
        op("t", lambda: g.tensor.matmul_mx(P[b][:, 0:w], lq, lp, rq, rp, start, stop), R, (), ["p%d" % b], ext=ext)

    def iota(out, pattern, base, cm, key):
        if key == "ip":
            op("g", lambda: g.iota(out, pattern, base, cm), (), [key])
        else:
            op("g", lambda: g.iota(out, pattern, base, cm, allow_small_or_imprecise_dtypes=True), (), [key])

    def lanes(r):
        sets = [topo.engines(T.cores[r], T.cores[(r + 1 + t) % n]) for t in range(ROUNDS)]
        return [e for e in sets[0] if all(e in s for s in sets)]

    op("s", lambda: g.sync.dma_start(T.us[:], T.u[:]), (), ["us"], dma="du")
    op("a", lambda: S.dma_start(T.xs[:], T.x[:]), (), ["xs"], dma="dx")

    iota(T.ip[:], [[0, 1]], 0, 1, "ip")
    iota(T.i16[:], [[16, 12]], 0, 0, "i16")
    iota(T.jm[:], [[0, 8], [1, 16]], 0, 0, "jm")
    iota(T.dd[:], [[-1, 128]], 0, 1, "dd")
    iota(T.kk[:], [[16, 8], [0, 16]], 0, 0, "kk")
    iota(T.j4[:], [[0, 32], [1, 4]], 0, 0, "j4")
    iota(T.i4[:], [[4, 128]], 0, 0, "i4")

    STK = ["st.a", "st.b"] + ["st.h%d" % b for b in range(4)]
    op("v", lambda: V.memset(T.bt[:], 0.0), (), ["bt%d" % k for k in range(8)])
    op("v", lambda: V.memset(T.et[:], 0.0), (), ["et"])
    op("v", lambda: V.memset(T.st[:, 320:512], 0.0), (), STK[2:])
    op("v", lambda: V.memset(T.off[:, 7:8], 0.0), (), ["off7"])

    ts(T.ci[:, 0:1], T.ip[:], 15, A_.bitwise_and, R=["ip"], W=["ci0"])
    ts(T.ci[:, 1:2], T.ip[:], 3, A_.bitwise_and, R=["ip"], W=["ci1"])
    ts(T.ci[:, 2:3], T.ip[:], 2, A_.logical_shift_right, 3, A_.bitwise_and, R=["ip"], W=["ci2"])
    ts(T.ci[:, 3:4], T.ip[:], 1, A_.logical_shift_right, 4, A_.bitwise_and, R=["ip"], W=["ci3"])
    ts(T.ci[:, 4:5], T.ip[:], 112, A_.bitwise_and, R=["ip"], W=["ci4"])
    cp("v", T.lu[:], T.i16[:, 0:8], ["i16"], ["lu"])
    cp("v", T.cf[:, 0:5], T.ci[:, 0:5], ["ci%d" % i for i in range(5)], ["cf"])
    cr, ct, ca, cq4, g16 = [T.cf[:, i:i + 1] for i in range(5)]
    col = {k: T.cd[:, i:i + 1] for i, k in enumerate(["c16", "c4", "q", "rq", "c192", "c224", "g32"])}
    lin(col["c16"], cr, -255.0, 3840.0, ["cf"], ["c16"])
    lin(col["c4"], ca, 1024.0, -3072.0, ["cf"], ["c4"])
    lin(col["q"], cq4, 1.0, ct, ["cf"], ["q"])
    lin(col["c192"], g16, 12.0, cr, ["cf"], ["c192"])
    lin(col["c224"], g16, 1.0, 224.0, ["cf"], ["c224"])
    lin(col["g32"], g16, 2.0, 0.0, ["cf"], ["g32"])
    lin(col["rq"], col["q"], -1.0, cr, ["cf", "q"], ["rq"])
    ts(T.et[:, 3:515:4], T.dd[:], 0.0, A_.is_equal, R=["dd", "et"], W=["et"])
    ts(T.mp[:], T.jm[:], cr, A_.not_equal, BIG, A_.mult, R=["jm", "cf"], W=["mp"])
    ts(T.ko[:], T.jm[:], cr, A_.is_le, 2 * BIG, A_.mult, R=["jm", "cf"], W=["ko"])
    for b in range(4):
        ts(T.gt[:, b:512:4], T.kk[:], g16, A_.is_equal, R=["kk", "cf"], W=["gt%d" % b])

    def quant_e(b):
        quant(T.eq[:, 128 * b:128 * b + 128], T.ep[:, 128 * b:128 * b + 128], T.et[:, 3 - b:515 - b], ["et"], ["eq%d" % b])

    quant(T.uq[:], T.up[:], T.us[:], ["us"], ["uq"])
    quant(T.xq[:], T.xp[:], T.xs[:], ["xs"], ["xq"])
    cp("v", T.ubq[:].bitcast(dt.uint32), T.uq[:].bitcast(dt.uint32).indirect(T.lu[:]), ["uq", "lu"], ["ubq"])
    cp("a", T.ubp[:], T.up[:].indirect(T.lu[:]), ["uq", "lu"], ["ubp"])
    UB = ["ubq", "ubp"]
    mm(6, 128, T.ubq[:], T.ubp[:], T.xq[:], T.xp[:], UB + ["xq"])
    mm(7, 128, T.ubq[:], T.ubp[:], T.xq[:], T.xp[:], UB + ["xq"])
    quant_e(0)
    quant_e(1)
    cp("a", T.sc[:], P[7][:, 0:128], (), ["sc"], ["p7"])
    op("s", lambda: g.sync.dma_start(T.wq[:].bitcast(dt.uint8), T.wc[:]), ["us", "xs"], ["wq"], dma="dwq")
    op("s", lambda: g.sync.dma_start(T.wp[:], T.ws[:]), (), ["wp"], dma="dwp")
    op("s", lambda: g.sync.dma_start(T.vs[:], T.v[:]), (), ["vs"], dma="dv")
    for t in range(ROUNDS):
        op("s", lambda t=t: g.sync.dma_start(T["lq%d" % t][:, M:C].bitcast(dt.uint8), T.xq[:, 0:KEEP].bitcast(dt.uint8)), ["xq"], (), dma="dpad")
        op("s", lambda t=t: g.sync.dma_start(T["lp%d" % t][:, M:C], T.xp[:, 0:KEEP]), ["xq"], (), dma="dpad")
    op("s", lambda: g.sync.dma_start(T.sp[:, 128:192], T.xp[:, 0:64]), ["xq"], ["pad"], dma="dpad")

    later = []

    def fill(k=1):
        for _ in range(k):
            if later:
                later.pop(0)()

    def unpack(qk, cq, cs, banks):
        for b in range(4):
            mm(banks[b], 128, T.eq[:, 128 * b:128 * b + 128], T.ep[:, 128 * b:128 * b + 128], cq, cs, ["eq%d" % b] + qk)

    def ranking(vold, vkey, places, shadow1=None, shadow2=None):
        scan(T.own[:], T.ko[:], T.xm[:], A_.add, A_.min, ["ko", "xm"], ["own"])
        if shadow1:
            shadow1()

        def bits(k):
            return T.bt[:, 512 * (k // 4) + 4 * (16 * k + 16) + k % 4:512 * (k // 4) + 512:4]

        def junk(k):
            return T.junk[:, 128 * k + 16 * k + 16:128 * k + 128]

        for k in range(KA, 7):
            op("a", lambda k=k: S.activation(junk(k), T.sc[:, 16 * k + 16:128], AF.Sign, bias=T.own[:, 16 * k + 15:16 * k + 16], scale=-1.0),
               ["sc", "own"], ["junk%d" % k])
        for k in range(KA, 7):
            op("a", lambda k=k: S.activation(bits(k), junk(k), AF.Relu, scale=-1.0, accum_out=T.off[:, k:k + 1]),
               ["junk%d" % k], ["bt%d" % k, "off%d" % k])
        for k in range(KA):
            ts(bits(k), T.sc[:, 16 * k + 16:128], T.own[:, 16 * k + 15:16 * k + 16], A_.is_gt, R=["sc", "own"], W=["bt%d" % k])
            op("a", lambda k=k: S.activation(junk(k), bits(k), AF.Copy, accum_out=T.off[:, k:k + 1]),
               ["bt%d" % k], ["off%d" % k, "junk%d" % k])
        tt(T.bt[:, 515:1024:4], T.sc[:], T.own[:], A_.is_gt, ["sc", "own"], ["bt7"])
        fill()
        quant(T.bq[:], T.bp[:], T.bt[:], ["bt%d" % k for k in range(8)], ["bq"])
        mm(6, 128, T.gq[:], T.gp[:], T.bq[:, 0:128], T.bp[:, 0:128], ["gq", "bq"], True, False)
        mm(6, 128, T.gq[:], T.gp[:], T.bq[:, 128:256], T.bp[:, 128:256], ["gq", "bq"], False, True)
        scan(T.dsc[:], T.kc[:], T.bt[:, 515:1024:4], A_.max, A_.add, ["kc", "bt7"], ["dsc"])
        if shadow2:
            shadow2()
        tt(T.rs[:], T.off[:], T.dsc[:, 15:128:16], A_.add, ["dsc"] + ["off%d" % k for k in range(8)], ["rs"])
        scan(T.sel[:], T.k16[:], P[6][:, 0:128], A_.add, A_.max, ["k16"], ["sel"], ["p6"])
        fill()
        tt(T.rr[:], T.rs[:], T.sel[:, 15:128:16], A_.subtract, ["rs", "sel"], ["rr"])
        fill()
        cp("v", T.lr[:], T.rr[:], ["rr"], ["lr"])
        fill()
        cp("v", T.wb[:].indirect(T.lr[:]), vold, ["lr", vkey], ["wb"])
        fill()
        scan(T.s4[:, 0:places], T.k4[:, 0:places], T.wb[:, 0:places], A_.add, A_.max, ["k4", "wb"], ["s4"])
        fill()
        ts(T.l32[:, 0:places // 4], T.s4[:, 3:places:4], col["c4"], A_.add, R=["s4", "c4"], W=["l32"])
        fill()

    def score_list():
        later[0:0] = [
            lambda: ts(T.m1[:], T.rr[:], float(NA), A_.is_ge, col["c224"], A_.mult, R=["rr", "c224"], W=["m1"]),
            lambda: ts(T.m2[:], T.rr[:], float(KEEP), A_.is_ge, 336.0, A_.mult, R=["rr"], W=["m2"]),
            lambda: tt(T.m3[:], T.m1[:], T.rr[:], A_.add, ["m1", "rr"], ["m3"]),
            lambda: tt(T.m4[:], T.m3[:], T.m2[:], A_.add, ["m3", "m2"], ["m4"]),
            lambda: ts(T.la[:], T.m4[:], col["g32"], A_.add, R=["m4", "g32"], W=["la"])]

    def consts1():
        quant_e(3)
        unpack(["xq"], T.xq[:], T.xp[:], [0, 1, 2, 3])

    def consts2():
        lin(T.i4t[:], T.i4[:], 1.0, ct, ["i4", "cf"], ["i4t"])
        ts(T.k16[:], T.mp[:], 65536.0 + 256.0, A_.min, -65536.0, A_.add, R=["mp"], W=["k16"])
        ts(T.k4a[:], T.j4[:], ca, A_.not_equal, 65536.0 + 1024.0, A_.mult, R=["j4", "cf"], W=["k4a"])
        lin(T.t2[:], T.jm[:, 0:128:2], 4.0, 0.0, ["jm"], ["t2"])
        lin(T.t3[:], T.jm[:, 0:128:2], 8.0, col["rq"], ["jm", "rq"], ["t3"])
        lin(T.k4[:], T.k4a[:], 1.0, -65536.0, ["k4a"], ["k4"])
        for b in range(4):
            cp("a", T.u0[:, b:512:4], P[b][:, 0:128], (), ["u0%d" % b], ["p%d" % b])
        later.extend([
            lambda: ts(T.t1[:], T.kk[:, 0:128:2], g16, A_.is_equal, 1000.0, A_.mult, R=["kk", "cf"], W=["t1"]),
            lambda: tt(T.t4[:], T.t1[:], T.t2[:], A_.add, ["t1", "t2"], ["t4"]),
            lambda: tt(T.t5[:], T.t4[:], T.t3[:], A_.min, ["t4", "t3"], ["t5"]),
            lambda: ts(T.lya[:], T.t5[:], col["q"], A_.add, R=["t5", "q"], W=["lya"]),
            lambda: ts(T.lsc[:], T.i16[:], col["c192"], A_.add, R=["i16", "c192"], W=["lsc"])])

    lin(T.kc[:], T.kk[:], 1.0, col["c16"], ["kk", "c16"], ["kc"])
    tt(T.xm[:], P[6][:, 0:128], T.mp[:], A_.add, ["mp"], ["xm"], ["p6"])
    quant_e(2)
    later.append(lambda: quant(T.gq[:], T.gp[:], T.gt[:], ["gt%d" % b for b in range(4)], ["gq"]))
    ranking(T.i4t[:], "i4t", C, consts1, consts2)

    UE = ["ue%d" % b for b in range(4)]
    UL = ["ul%d" % b for b in range(4)]
    U0 = ["u0%d" % b for b in range(4)]
    cp("v", T.ust[:, 0:256], T.u0[:].indirect(T.l32[:, 0:16]), U0 + ["l32"], ["ue0", "ue1"])
    cp("a", T.ust[:, 256:512], T.u0[:].indirect(T.l32[:, 16:32]), U0 + ["l32"], ["ue2", "ue3"] + UL)

    vbuf = [("va", T.va), ("vb", T.vb)]

    def early_build(first):
        src = ["ue0", "ue1"] if first else UE
        D = ["dup0", "dup1"]
        cp("v", T.dup[:, 0:96:2, :], T.ust[:, 64:256], src, ["dup0"])
        cp("v" if first else "a", T.dup[:, 1:96:2, :], T.ust[:, 64:256], src, ["dup1"])
        fill()
        for i in range(2):
            cp("a" if first else "g", T.yc[:, 192 * i:192 * i + 192], T.dup[:, 48:96, :], D, ["yc0.%d" % i])
        for i in (1, 2):
            cp("g", T.yc[:, 384 * i:384 * i + 384], T.yc[:, 0:384], ["yc0.0", "yc0.1"], ["yc%d" % i])
        for i in range(8):
            cp("v" if first or i < NV else "a", T.yb[:, 192 * i:192 * i + 192], T.dup[:, 0:48, :], D, ["yb%d" % i])
        cp("a", T.ya[:], T.ust[:, 0:128].indirect(T.lya[:]), src + ["lya"], ["ya"])
        YB = ["yb%d" % i for i in range(8)]
        fill()
        cp("v", T.yb[:].indirect(T.lsc[:]), T.ust[:, 128:320], UE + ["lsc"] + YB, YB)
        fill()
        quant(T.yq[:, 256:640], T.yp[:, 256:640], T.yb[:], YB, ["yqb"])

    def last_base():
        cp("a", T.yc[:, 1152:1536], T.yc[:, 0:384], ["yc0.0", "yc0.1"], ["yc3"])

    def quant_a():
        quant(T.yq[:, 0:256], T.yp[:, 0:256], T.ya[:], ["ya"], ["yqa"])

    def early_products():
        mm(4, 384, T.ubq[:], T.ubp[:], T.yq[:, 256:640], T.yp[:, 256:640], UB + ["yqb"])
        mm(5, 256, T.ubq[:], T.ubp[:], T.yq[:, 0:256], T.yp[:, 0:256], UB + ["yqa"])

    def early_evac():
        cp("a", T.ps[:, 256:640], P[4][:, 0:384], (), ["psb"], ["p4"])
        cp("a", T.ps[:, 0:256], P[5][:, 0:256], (), ["psa"], ["p5"])

    def late_trials():
        K = ["yc0.0", "yc0.1", "yc1", "yc2", "yc3"]
        a, b, c = 640, 640 + CUT, 1024
        cp("v", T.yc[:].indirect(T.lsc[:]), T.ust[:, 320:512], UL + ["lsc"] + K, K)
        fill()
        quant(T.yq[:, a:b], T.yp[:, a:b], T.yc[:, 0:4 * CUT], K, ["yqc"])
        mm(6, b - a, T.ubq[:], T.ubp[:], T.yq[:, a:b], T.yp[:, a:b], UB + ["yqc"])
        quant(T.yq[:, b:c], T.yp[:, b:c], T.yc[:, 4 * CUT:1536], K, ["yqd"])
        mm(7, c - b, T.ubq[:], T.ubp[:], T.yq[:, b:c], T.yp[:, b:c], UB + ["yqd"])
        cp("a", T.ps[:, a:b], P[6][:, 0:b - a], (), ["psc"], ["p6"])
        fill(9)
        cp("v", T.ps[:, b:c], P[7][:, 0:c - b], (), ["psd"], ["p7"])
        PS = ["psa", "psb", "psc", "psd"]
        cp("a", T.sc[:], T.ps[:].indirect(T.la[:]), PS + ["la"], ["sc"])
        tt(T.xm[:], T.ps[:].indirect(T.la[:]), T.mp[:], A_.add, PS + ["la", "mp"], ["xm"])

    def new_v(i):
        cp("a", vbuf[i][1][:], T.i4t[:].indirect(T.lr[:]), ["i4t", "lr"], [vbuf[i][0]])

    score_list()
    fill()
    early_build(True)
    last_base()
    quant_a()
    early_products()
    early_evac()
    new_v(0)
    late_trials()

    eng = lanes(rank)
    half = len(eng) // 2
    masks = [sum(1 << e for e in eng[:half]), sum(1 << e for e in eng[half:2 * half])]
    for t in range(ROUNDS):
        last = t == ROUNDS - 1
        ranking(vbuf[t % 2][1][:], vbuf[t % 2][0], KEEP)
        w = 6 if last else 10
        cp("v", T.st[:, 0:16 * w], T.ust[:].indirect(T.l32[:, 0:w]), UE + UL + ["l32"], ["st.a"])
        cp("a", T.st[:, 16 * w:32 * w], T.ust[:].indirect(T.l32[:, w:2 * w]), UE + UL + ["l32"], ["st.b"])
        quant(T.sq[:, 0:128], T.sp[:, 0:128], T.st[:], STK, ["sq"])
        rid, pid = topo.addr(T.cores[(rank + 1 + t) % n], core)
        lq, lp, arr = T["lq%d" % t], T["lp%d" % t], "arr%d" % t
        xf = [RemoteDMATransfer(dst_ids=[DstId(rid=rid, pnc=pid)], dma_engine_mask=masks[0], remote_sem=T.sem[arr],
                                src=T.sq[:, 0:M].bitcast(dt.uint8), dst=lq[:, 128:128 + M].bitcast(dt.uint8)),
              RemoteDMATransfer(dst_ids=[DstId(rid=rid, pnc=pid)], dma_engine_mask=masks[1], remote_sem=T.sem[arr],
                                src=T.sp[:, 0:4 * M], dst=lp[:, 128:128 + 4 * M])]
        op("g", lambda xf=xf: g.remote_dma_fused(xf, local_sem=T.sem.sent), ["sq", "pad"], (), remote=("sent", 2 * half))
        if last:
            cp("a", T.st[:, 192:320], T.ust[:].indirect(T.l32[:, 12:20]), UE + UL + ["l32"], ["st.b"])
        new_v((t + 1) % 2)
        if not last:
            unpack(["sq"], T.sq[:, 0:128], T.sp[:, 0:128], [0, 1, 2, 3])
            score_list()
            fill(3)
            for b in range(4):
                cp("a" if b % 2 == 0 else "v", T.ust[:, b:320:4], P[b][:, 0:KEEP], (), ["ue%d" % b], ["p%d" % b])
            early_build(False)
        else:
            vk, vn = vbuf[(t + 1) % 2]
            quant(T.vq[:], T.vp[:], T.vs[:], ["vs"], ["vq"])
            lin(T.ic[:], T.i4[:], 0.25, 0.0, ["i4"], ["ic"])
            scan(T.s4[:], T.k4[:], vn[:], A_.add, A_.max, ["k4", vk], ["s4"])
            cp("v", T.ob[:].indirect(T.lr[:]), T.ic[:], ["lr", "ic"], ["ob"])
            ts(T.lf[:], T.s4[:, 3:128:4], col["c4"], A_.add, R=["s4", "c4"], W=["lf"])
            op("s", lambda: g.sync.dma_start(T.ol[:], T.ob[0:128:16, :]), ["ob"], (), dma="dout")
        got = len(lanes((rank - 1 - t) % n)) // 2 * 2
        for b in range(4):
            mm(4 + b, 128, T.wq[:, 128 * b:128 * b + 128], T.wp[:, 128 * b:128 * b + 128], lq[:, M:M + 128], lp[:, M:M + 128],
               ["wq", "wp", "pad"], ext=[(arr, got)])
            mm(b, 128, T.eq[:, 128 * b:128 * b + 128], T.ep[:, 128 * b:128 * b + 128], lq[:, M:M + 128], lp[:, M:M + 128],
               ["eq%d" % b, "pad"])
        for b in range(4):
            op("a", lambda b=b: S.activation(T.rl[:, M * b:M * b + M], P[4 + b][:, KEEP:C], AF.Relu, scale=0.03125),
               (), ["rl%d" % b], ["p%d" % (4 + b)])
            tt(T.st[:, 320 + b:512:4], T.rl[:, M * b:M * b + M], P[b][:, KEEP:C], A_.add, ["rl%d" % b], ["st.h%d" % b], ["p%d" % b])
        if not last:
            quant(T.hq[:], T.hp[:], T.st[:], STK, ["hq"])
            last_base()
            unpack(["hq"], T.hq[:], T.hp[:], [0, 1, 2, 3])
            quant_a()
            early_products()
            for b in range(4):
                cp("a" if b % 2 == 0 else "v", T.ust[:, 320 + b:512:4], P[b][:, KEEP:C], (), ["ul%d" % b], ["p%d" % b])
            early_evac()
            late_trials()

    cp("v", T.fin[:, 0:256], T.st[:].indirect(T.lf[:, 0:16]), STK + ["lf"], ["fin0"])
    cp("a", T.fin[:, 256:512], T.st[:].indirect(T.lf[:, 16:32]), STK + ["lf"], ["fin1"])
    quant(T.fq[:], T.fp[:], T.fin[:], ["fin0", "fin1"], ["fq"])
    mm(0, 128, T.vq[:], T.vp[:], T.fq[:], T.fp[:], ["vq", "fq"])
    op("s", lambda: g.sync.dma_start(T.oc[:], T.fq[:].bitcast(dt.uint8)), ["fq"], (), dma="dout")
    for k in range(4):
        q = "a" if k < 2 else "s"
        op(q, lambda k=k, q=q: Q[q].dma_start(T.osc[4 * k:4 * k + 4, :], T.fp[32 * k:32 * k + 4, :]), ["fq"], (), dma="dout")
    cp("v", T.ysb[:], P[0][:, 0:128], (), ["ysb"], ["p0"])
    op("a", lambda: S.dma_start(T.y[:], T.ysb[:]), ["ysb"], (), dma="dout")
    for sem in SEMAPHORES:
        if sem in count:
            need("g", (sem, count[sem], {}))
